import numpy as np
import ml_dtypes


def mxq(x, axis, fmt="e4m3"):
    dtype, down = {"e4m3": (ml_dtypes.float8_e4m3fn, 7), "e5m2": (ml_dtypes.float8_e5m2, 14)}[fmt]
    v = np.moveaxis(np.asarray(x, np.float32).astype(ml_dtypes.bfloat16).astype(np.float64), axis, -1)
    blocks = v.reshape(v.shape[:-1] + (-1, 32))
    amax = np.abs(blocks).max(-1, keepdims=True)
    byte = np.maximum(np.where(amax > 0, np.frexp(amax)[1] - 1 + 127, 0) - down, 1)
    scale = np.exp2(byte - 127.0)
    codes = (blocks / scale).astype(np.float32).astype(dtype).astype(np.float64)
    return np.moveaxis((codes * scale).reshape(v.shape), -1, axis)


WIDE = False


def mx_kscale(k):
    if not WIDE:
        return np.ones(k)
    levels = np.array([10, -10, 5, -5, 0])
    if k % 512:
        return np.exp2(np.random.permutation(np.resize(levels, k // 32))).repeat(32)
    a = np.empty((k // 512, 16))
    for p in range(k // 512):
        a[p, :8] = np.random.permutation(np.resize(levels, 8))
        for g in range(8):
            far = levels[np.abs(levels - a[p, g]) >= 10]
            a[p, g + 8] = far[np.random.randint(len(far))]
    return np.exp2(a.ravel()).repeat(32)


def f64(x):
    return np.asarray(x).astype(np.float64)


def striped(idx):
    return np.tile(idx.reshape(-1, 16).T, (8, 1)).astype(np.uint16)


def unstriped(offs):
    return offs[:16].T.reshape(-1).astype(np.int64)


E2M1 = np.array([0.0, 0.5, 1.0, 1.5, 2.0, 3.0, 4.0, 6.0, -0.0, -0.5, -1.0, -1.5, -2.0, -3.0, -4.0, -6.0])


def pack_weight(w, fmt):
    k, n = w.shape
    w = f64(np.asarray(w, np.float32).astype(ml_dtypes.bfloat16)).reshape(k // 32, 32, n)
    amax = np.abs(w).max(1)
    if fmt == "e4m3":
        byte = np.frexp(amax)[1] - 1 + 127 - 7
    else:
        mant, ex = np.frexp(amax / 6.0)
        byte = np.where(mant > 0.5, ex, ex - 1) + 127
    byte = np.clip(np.where(amax > 0, byte, 1), 1, 254)
    scaled = (w * np.exp2(127.0 - byte)[:, None, :]).reshape(k, n).astype(np.float32)
    by_word = np.ascontiguousarray(scaled.reshape(k // 512, 128, 4, n).transpose(0, 1, 3, 2))
    if fmt == "e4m3":
        words = by_word.astype(ml_dtypes.float8_e4m3fn).view(np.uint8)
    else:
        c = by_word.astype(ml_dtypes.float4_e2m1fn).view(np.uint8) & 0xF
        words = (c[..., 0::2] | (c[..., 1::2] << 4)).reshape(k // 512, 128, 2 * n)
    return np.ascontiguousarray(words), np.ascontiguousarray(byte.astype(np.uint8).reshape(k // 512, 16, n))


def unpack_weight(words, scales, fmt):
    g, _, n = scales.shape
    words = np.ascontiguousarray(words).reshape(g, 128, n, -1)
    if fmt == "e4m3":
        vals = words.view(ml_dtypes.float8_e4m3fn).astype(np.float64)
    else:
        nib = np.empty((g, 128, n, 4), np.uint8)
        nib[..., 0::2] = words & 0xF
        nib[..., 1::2] = words >> 4
        vals = E2M1[nib]
    vals = vals * np.repeat(np.exp2(scales.astype(np.float64) - 127.0), 8, axis=1)[..., None]
    return vals.transpose(0, 1, 3, 2).reshape(g * 512, n)


def gelu(v):
    return 0.5 * v * (1.0 + np.tanh(np.sqrt(2.0 / np.pi) * (v + 0.044715 * v**3)))


def twice(P):
    return np.random.permutation(np.repeat(np.arange(P), 2))


def bf(x):
    return np.asarray(x, np.float32).astype(ml_dtypes.bfloat16)


def planes(Y):
    n, m = Y.shape
    b = f64(bf(Y)).reshape(n // 32, 32, m)
    amax = np.abs(b).max(1)
    byte = np.clip(np.where(amax > 0, np.frexp(amax)[1] - 1 + 127 - 7, 1), 1, 254)
    codes = (b * np.exp2(127.0 - byte)[:, None, :]).reshape(n, m).astype(np.float32).astype(ml_dtypes.float8_e4m3fn).view(np.uint8)
    words = codes.reshape(n // 512, 128, 4, m).transpose(0, 1, 3, 2)
    return np.ascontiguousarray(words), np.ascontiguousarray(byte.astype(np.uint8).reshape(n // 512, 16, m))


K, T, S, P, H = 1536, 4096, 1024, 512, 1024


def setup_inputs():
    n = np.random.standard_normal
    s = mx_kscale(K)[:, None]
    u = mx_kscale(H)[:, None]
    d = {}
    d["tab_words"], d["tab_scales"] = pack_weight(n((K, T)) * s, "e4m3")
    d["offs"] = striped(np.random.permutation(T)[:S])
    d["pos1"] = striped(np.random.permutation(S)[:P])
    d["pos2"] = striped(np.random.permutation(S)[:P])
    d["pos3"] = striped(twice(P))
    d["w4_words"], d["w4_scales"] = pack_weight(n((K, H)) / K ** 0.5 / s * u.T, "e2m1")
    d["w2"] = (0.6 * n((H, H)) / H ** 0.5 / u * np.exp(0.8 * n(H))[None, :]).astype(np.float32)
    d["gain"] = (1.6 * np.exp(0.3 * n(H)) / u[:, 0]).astype(np.float32)
    return d


def reference(tab_words, tab_scales, offs, pos1, pos2, pos3, w4_words, w4_scales, w2, gain):
    v = unpack_weight(tab_words, tab_scales, "e4m3")[:, unstriped(offs)]
    w4 = unpack_weight(w4_words, w4_scales, "e2m1")
    h = w4.T @ v
    hs = h * f64(gain)[:, None]
    x = mxq(h[:, unstriped(pos1)] + h[:, unstriped(pos2)], 0, "e4m3")
    beat = np.abs(hs[:, unstriped(pos1)] - hs[:, unstriped(pos2)])
    pair = (mxq(f64(w2), 0, "e4m3").T @ x) + beat
    y = pair[:, unstriped(pos3)] - np.tanh(hs)
    words, scales = planes(y)
    return y, words, scales

@@ -1,0 +1,236 @@
+from contextlib import ExitStack
+
+import concourse.mybir as mybir
+
+K, T, S, PAIRS, H = 1536, 4096, 1024, 512, 1024
+FLOPS = 2 * K * H * S + 2 * H * H * PAIRS
+
+F32 = mybir.dt.float32
+BF16 = mybir.dt.bfloat16
+I32 = mybir.dt.int32
+U32 = mybir.dt.uint32
+U16 = mybir.dt.uint16
+U8 = mybir.dt.uint8
+FP8X4 = mybir.dt.float8_e4m3fn_x4
+FP4X4 = mybir.dt.float4_e2m1fn_x4
+ACT = mybir.ActivationFunctionType
+ALU = mybir.AluOpType
+
+P = 128
+PACK = 4
+K_PASS = P * PACK
+PASSES = K // K_PASS
+GROUPS = H // K_PASS
+BANK = 512
+QUADS = 4
+PER_COLUMN = 16
+SPARE = 32
+HALF = PAIRS // 2
+ROW0 = P - 16 * PASSES
+Y_PIECES = [(0, 0, 512), (0, 512, 512), (1, 0, 512), (1, 512, 256), (1, 768, 256)]
+
+
+def tile_list_musette_reed_beating_kernel(
+    tc, tab_words, tab_scales, offs, pos1, pos2, pos3, w4_words, w4_scales, w2, gain, out_0, out_1, out_2
+):
+    nc = tc.nc
+    with ExitStack() as ctx:
+        lists = ctx.enter_context(tc.tile_pool(name="lists", bufs=1))
+        keep = ctx.enter_context(tc.tile_pool(name="keep", bufs=1))
+        big = ctx.enter_context(tc.tile_pool(name="big", bufs=3))
+        rows = ctx.enter_context(tc.tile_pool(name="rows", bufs=8))
+        stage = ctx.enter_context(tc.tile_pool(name="stage", bufs=4))
+        psum = ctx.enter_context(tc.psum_pool(name="psum", bufs=8))
+
+        idx = lists.tile([P, S // PER_COLUMN], U16, name="idx")
+        p1 = lists.tile([P, PAIRS // PER_COLUMN], U16, name="p1")
+        p2 = lists.tile([P, PAIRS // PER_COLUMN], U16, name="p2")
+        p3 = lists.tile([P, S // PER_COLUMN], U16, name="p3")
+        nc.sync.dma_start(idx[:], offs)
+
+        tab_rows = big.tile([P, T], U8, name="tab_rows", tag="big", align_bytes=64)
+        nc.vector.memset(tab_rows[:ROW0, :].bitcast(I32), 0)
+        nc.sync.dma_start(tab_rows[ROW0:, :].bitcast(I32), tab_scales.rearrange("a q c -> q a c").bitcast(I32))
+        w4_rows = keep.tile([P, H], U8, name="w4_rows")
+        nc.vector.memset(w4_rows[:ROW0, :].bitcast(I32), 0)
+        nc.sync.dma_start(w4_rows[ROW0:, :].bitcast(I32), w4_scales.rearrange("a q c -> q a c").bitcast(I32))
+        w4_raw = keep.tile([P, PASSES, 2 * H], U8, name="w4_raw")
+        nc.sync.dma_start(w4_raw[:].bitcast(I32), w4_words.rearrange("a p c -> p a c").bitcast(I32))
+
+        def load_table(a):
+            words = big.tile([P, T], I32, name="tab%d" % a, tag="big", align_bytes=64)
+            nc.sync.dma_start(words[:], tab_words[a].rearrange("p t i -> p (t i)").bitcast(I32))
+            return words
+
+        table = [load_table(0)]
+        for tile, source in ((p1, pos1), (p2, pos2), (p3, pos3)):
+            nc.sync.dma_start(tile[:], source)
+        gains = keep.tile([P, GROUPS, PACK], F32, name="gains")
+        nc.sync.dma_start(gains[:], gain.rearrange("(g p t) -> p g t", g=GROUPS, t=PACK))
+        table.extend([load_table(1), load_table(2)])
+        minus_gains = keep.tile([P, GROUPS, PACK], F32, name="minus_gains")
+        nc.gpsimd.tensor_scalar(minus_gains[:], gains[:], -1.0, 0.0, ALU.mult, ALU.add)
+        slices = [(g, t) for g in range(GROUPS) for t in range(PACK)]
+        pair = {}
+        for g, t in slices:
+            pair[g, t] = keep.tile([P, PAIRS + SPARE], F32, name="pair%d%d" % (g, t))
+            nc.gpsimd.memset(pair[g, t][:, PAIRS:], 0.0)
+
+        def spread_rows(queue, packed, name):
+            planes = keep.tile([P, PASSES, packed.shape[1]], U8, name=name, align_bytes=64)
+            nc.gpsimd.memset(planes[:].rearrange("p a c -> p (a c)").bitcast(I32), 0)
+            for q in range(QUADS):
+                first_row = ROW0 + 4 * PASSES * q
+                queue.dma_start(
+                    planes[32 * q : 32 * q + 4, :, :].bitcast(I32),
+                    packed[first_row : first_row + 4 * PASSES, :].bitcast(I32),
+                )
+            return planes
+
+        w4_dealt = keep.tile([P, H], U8, name="w4_dealt")
+        nc.vector.tensor_copy(
+            w4_dealt[:].rearrange("p (t c) -> p t c", t=PACK), w4_rows[:].rearrange("p (c t) -> p t c", t=PACK)
+        )
+        w4_planes = spread_rows(nc.gpsimd, w4_dealt, "w4_planes")
+        v_rows = keep.tile([P, S], U8, name="v_rows")
+        nc.vector.tensor_copy(v_rows[:], tab_rows[:].indirect(idx[:]))
+        v_scales = spread_rows(nc.scalar, v_rows, "v_scales")
+
+        w4_codes = [
+            keep.tile([P, 2 * H], U8, name="w4_codes%d" % a, tag="w4_codes%d" % a, align_bytes=64) for a in range(PASSES)
+        ]
+        for a in range(PASSES):
+            nc.vector.tensor_copy(
+                w4_codes[a][:].bitcast(U16).rearrange("p (t c) -> p t c", t=PACK),
+                w4_raw[:, a, :].bitcast(U16).rearrange("p (c t) -> p t c", t=PACK),
+            )
+
+        v_words = []
+        for a in range(PASSES):
+            picked = rows.tile([P, S], U32, name="v_words%d" % a, tag="rows", align_bytes=64)
+            width = BANK if a == PASSES - 1 else S
+            for j0 in range(0, S, width):
+                nc.vector.tensor_copy(
+                    picked[:, j0 : j0 + width],
+                    table[a][:].bitcast(U32).indirect(idx[:, j0 // PER_COLUMN : (j0 + width) // PER_COLUMN]),
+                )
+            v_words.append(picked)
+
+        w2_raw = []
+        for g in range(GROUPS):
+            raw = big.tile([P, PACK, H], F32, name="w2_raw%d" % g, tag="big", align_bytes=64)
+            nc.sync.dma_start(raw[:], w2[g * K_PASS : (g + 1) * K_PASS, :].rearrange("(p j) n -> p j n", j=PACK))
+            w2_raw.append(raw)
+
+        h, first = {}, {}
+        x_codes = [keep.tile([P, PAIRS], U32, name="x_codes%d" % g, align_bytes=64) for g in range(GROUPS)]
+        x_scales = [keep.tile([P, PAIRS], U8, name="x_scales%d" % g, align_bytes=64) for g in range(GROUPS)]
+        for g in range(GROUPS):
+            first[g] = keep.tile([P, PACK, PAIRS], F32, name="first%d" % g)
+            second = keep.tile([P, PACK, PAIRS], F32, name="second%d" % g)
+            for t in range(PACK):
+                h[g, t] = keep.tile([P, S], F32, name="h%d%d" % (g, t))
+                c0 = (t * GROUPS + g) * P
+                for j0 in range(0, S, BANK):
+                    acc = psum.tile([P, BANK], F32, name="acc1", tag="acc")
+                    for a in range(PASSES):
+                        nc.tensor.matmul_mx(
+                            acc[:],
+                            lhsT=w4_codes[a][:, 2 * c0 : 2 * (c0 + P)].bitcast(FP4X4),
+                            lhsT_scale=w4_planes[:, a, c0 : c0 + P],
+                            rhs=v_words[a][:, j0 : j0 + BANK].bitcast(FP8X4),
+                            rhs_scale=v_scales[:, a, j0 : j0 + BANK],
+                            start=(a == 0),
+                            stop=(a == PASSES - 1),
+                        )
+                    nc.scalar.copy(h[g, t][:, j0 : j0 + BANK], acc[:])
+                halves = [slice(m0, m0 + HALF) for m0 in range(0, PAIRS, HALF)]
+                for m in halves:
+                    entries = slice(m.start // PER_COLUMN, m.stop // PER_COLUMN)
+                    nc.vector.tensor_copy(first[g][:, t, m], h[g, t][:].indirect(p1[:, entries]))
+                for m in halves:
+                    entries = slice(m.start // PER_COLUMN, m.stop // PER_COLUMN)
+                    nc.vector.tensor_tensor(
+                        second[:, t, m], h[g, t][:].indirect(p2[:, entries]), first[g][:, t, m], ALU.add
+                    )
+            x_bf = keep.tile([P, PAIRS, PACK], BF16, name="x_bf%d" % g, tag="w4_codes%d" % (2 if g == 0 else 9), align_bytes=64)
+            woven = x_bf[:].rearrange("p (c i) t -> p c t i", i=4)
+            planes = second[:].rearrange("p t (c i) -> p c t i", i=4)
+            if g == GROUPS - 1:
+                nc.vector.tensor_copy(woven, planes)
+            else:
+                nc.scalar.copy(woven, planes)
+            nc.vector.quantize_mx(x_codes[g][:].bitcast(FP8X4), x_scales[g][:], x_bf[:].rearrange("p m t -> p (m t)"))
+            for m in halves:
+                nc.vector.scalar_tensor_tensor(
+                    first[g][:, :, m], first[g][:, :, m], -2.0, second[:, :, m], ALU.mult, ALU.add
+                )
+
+        w2_codes, w2_scales = {}, {}
+        for out_g in range(GROUPS):
+            for g in range(GROUPS):
+                w2_bf = stage.tile([P, PACK, P, PACK], BF16, name="w2_bf", tag="stage", align_bytes=64)
+                nc.scalar.copy(
+                    w2_bf[:].rearrange("p t m j -> p m j t"),
+                    w2_raw[g][:, :, out_g * K_PASS : (out_g + 1) * K_PASS].rearrange("p j (m t) -> p m j t", t=PACK),
+                )
+                codes = keep.tile([P, K_PASS], U32, name="w2_codes%d%d" % (g, out_g), align_bytes=64)
+                scales = keep.tile([P, K_PASS], U8, name="w2_scales%d%d" % (g, out_g), align_bytes=64)
+                nc.vector.quantize_mx(codes[:].bitcast(FP8X4), scales[:], w2_bf[:].rearrange("p t m j -> p (t m j)"))
+                w2_codes[g, out_g], w2_scales[g, out_g] = codes, scales
+
+        bounded = {}
+        for g in range(GROUPS):
+            for t in range(PACK):
+                nc.scalar.activation(pair[g, t][:, :PAIRS], first[g][:, t, :], ACT.Abs, scale=gains[:, g, t : t + 1])
+            for t in range(PACK):
+                bounded[g, t] = rows.tile([P, S], F32, name="bounded%d%d" % (g, t), tag="rows", align_bytes=64)
+                nc.scalar.activation(bounded[g, t][:], h[g, t][:], ACT.Tanh, scale=minus_gains[:, g, t : t + 1])
+
+        y_codes = [keep.tile([P, S], U32, name="y_codes%d" % g, align_bytes=64) for g in range(GROUPS)]
+        y_scales = [keep.tile([P, S], U8, name="y_scales%d" % g, align_bytes=64) for g in range(GROUPS)]
+        y_rows = out_0.rearrange("(g p t) j -> g t p j", g=GROUPS, t=PACK)
+        for g, j0, width in Y_PIECES:
+            cols = slice(j0, j0 + width)
+            y = big.tile([P, PACK, width], F32, name="y", tag="big", align_bytes=64)
+            for t in range(PACK):
+                if j0 == 0:
+                    acc = psum.tile([P, BANK], F32, name="acc2", tag="acc")
+                    for r in range(GROUPS):
+                        nc.tensor.matmul_mx(
+                            acc[:],
+                            lhsT=w2_codes[r, g][:, t * P : (t + 1) * P].bitcast(FP8X4),
+                            lhsT_scale=w2_scales[r, g][:, t * P : (t + 1) * P],
+                            rhs=x_codes[r][:].bitcast(FP8X4),
+                            rhs_scale=x_scales[r][:],
+                            start=(r == 0),
+                            stop=(r == GROUPS - 1),
+                        )
+                    nc.vector.tensor_tensor(pair[g, t][:, :PAIRS], acc[:], pair[g, t][:, :PAIRS], ALU.add)
+            for t in range(PACK):
+                nc.vector.tensor_tensor(
+                    y[:, t, :],
+                    pair[g, t][:].indirect(p3[:, j0 // PER_COLUMN : (j0 + width) // PER_COLUMN]),
+                    bounded[g, t][:, cols],
+                    ALU.add,
+                )
+                nc.sync.dma_start(y_rows[g, t, :, cols], y[:, t, :])
+            y_bf = stage.tile([P, width, PACK], BF16, name="y_bf", tag="stage", align_bytes=64)
+            woven = y_bf[:].rearrange("p (c i) t -> p c t i", i=4)
+            planes = y[:].rearrange("p t (c i) -> p c t i", i=4)
+            if (g, j0, width) == Y_PIECES[-1]:
+                nc.vector.tensor_copy(woven, planes)
+            else:
+                nc.scalar.copy(woven, planes)
+            nc.vector.quantize_mx(
+                y_codes[g][:, cols].bitcast(FP8X4), y_scales[g][:, cols], y_bf[:].rearrange("p m t -> p (m t)")
+            )
+            nc.sync.dma_start(
+                out_1[g].rearrange("p m t -> p (m t)").bitcast(I32)[:, cols], y_codes[g][:, cols].bitcast(I32)
+            )
+            if j0 + width == S:
+                for q in range(QUADS):
+                    queue = nc.scalar if q % 2 else nc.sync
+                    queue.dma_start(
+                        out_2[g, 4 * q : 4 * q + 4, :].bitcast(I32), y_scales[g][32 * q : 32 * q + 4, :].bitcast(I32)
+                    )

@@ -37,7 +37,7 @@ def tile_list_musette_reed_beating_kernel(
     with ExitStack() as ctx:
         lists = ctx.enter_context(tc.tile_pool(name="lists", bufs=1))
         keep = ctx.enter_context(tc.tile_pool(name="keep", bufs=1))
-        big = ctx.enter_context(tc.tile_pool(name="big", bufs=3))
+        big = ctx.enter_context(tc.tile_pool(name="big", bufs=1))
         rows = ctx.enter_context(tc.tile_pool(name="rows", bufs=8))
         stage = ctx.enter_context(tc.tile_pool(name="stage", bufs=4))
         psum = ctx.enter_context(tc.psum_pool(name="psum", bufs=8))
@@ -46,28 +46,68 @@ def tile_list_musette_reed_beating_kernel(
         p1 = lists.tile([P, PAIRS // PER_COLUMN], U16, name="p1")
         p2 = lists.tile([P, PAIRS // PER_COLUMN], U16, name="p2")
         p3 = lists.tile([P, S // PER_COLUMN], U16, name="p3")
-        nc.sync.dma_start(idx[:], offs)
-
-        tab_rows = big.tile([P, T], U8, name="tab_rows", tag="big", align_bytes=64)
+        tab_rows = big.tile([P, T], U8, name="tab_rows", tag="slot2", align_bytes=64)
         nc.vector.memset(tab_rows[:ROW0, :].bitcast(I32), 0)
-        nc.sync.dma_start(tab_rows[ROW0:, :].bitcast(I32), tab_scales.rearrange("a q c -> q a c").bitcast(I32))
-        w4_rows = keep.tile([P, H], U8, name="w4_rows")
-        nc.vector.memset(w4_rows[:ROW0, :].bitcast(I32), 0)
-        nc.sync.dma_start(w4_rows[ROW0:, :].bitcast(I32), w4_scales.rearrange("a q c -> q a c").bitcast(I32))
-        w4_raw = keep.tile([P, PASSES, 2 * H], U8, name="w4_raw")
-        nc.sync.dma_start(w4_raw[:].bitcast(I32), w4_words.rearrange("a p c -> p a c").bitcast(I32))
+        nc.scalar.dma_start(tab_rows[ROW0:, :].bitcast(I32), tab_scales.rearrange("a q c -> q a c").bitcast(I32))
+        w4_first = big.tile([P, 2 * H], U8, name="w4_first", tag="slot1", align_bytes=64)
+        nc.sync.dma_start(w4_first[:].bitcast(I32), w4_words[0].bitcast(I32))
+        for tile, source in ((idx, offs), (p1, pos1), (p2, pos2), (p3, pos3)):
+            nc.sync.dma_start(tile[:], source)
+        gains = keep.tile([P, GROUPS, PACK], F32, name="gains")
+        nc.sync.dma_start(gains[:], gain.rearrange("(g p t) -> p g t", g=GROUPS, t=PACK))
 
         def load_table(a):
-            words = big.tile([P, T], I32, name="tab%d" % a, tag="big", align_bytes=64)
+            words = big.tile([P, T], I32, name="tab%d" % a, tag="slot%d" % a, align_bytes=64)
             nc.sync.dma_start(words[:], tab_words[a].rearrange("p t i -> p (t i)").bitcast(I32))
             return words
 
         table = [load_table(0)]
-        for tile, source in ((p1, pos1), (p2, pos2), (p3, pos3)):
-            nc.sync.dma_start(tile[:], source)
-        gains = keep.tile([P, GROUPS, PACK], F32, name="gains")
-        nc.sync.dma_start(gains[:], gain.rearrange("(g p t) -> p g t", g=GROUPS, t=PACK))
-        table.extend([load_table(1), load_table(2)])
+        w4_rest = stage.tile([P, PASSES - 1, 2 * H], U8, name="w4_rest", tag="stage", align_bytes=64)
+        nc.sync.dma_start(w4_rest[:].bitcast(I32), w4_words[1:].rearrange("a p c -> p a c").bitcast(I32))
+        w4_raw = [w4_first[:], w4_rest[:, 0, :], w4_rest[:, 1, :]]
+        w4_rows = keep.tile([P, PASSES, H], U8, name="w4_rows")
+        nc.gpsimd.memset(w4_rows[:].rearrange("p a c -> p (a c)").bitcast(I32), 0)
+        for q in range(QUADS):
+            queue = nc.gpsimd if q == QUADS - 1 else nc.sync
+            queue.dma_start(
+                w4_rows[32 * q : 32 * q + 4, :, :].bitcast(I32),
+                w4_scales[:, 4 * q : 4 * q + 4, :].rearrange("a r c -> r a c").bitcast(I32),
+            )
+
+        w4_codes = [
+            keep.tile([P, 2 * H], U8, name="w4_codes%d" % a, tag="w4_codes%d" % a, align_bytes=64) for a in range(PASSES)
+        ]
+
+        def deal_words(a):
+            nc.vector.tensor_copy(
+                w4_codes[a][:].bitcast(U16).rearrange("p (t c) -> p t c", t=PACK),
+                w4_raw[a].bitcast(U16).rearrange("p (c t) -> p t c", t=PACK),
+            )
+
+        deal_words(0)
+        table.append(load_table(1))
+
+        v_rows = keep.tile([P, S], U8, name="v_rows")
+        nc.vector.tensor_copy(v_rows[:], tab_rows[:].indirect(idx[:]))
+        v_scales = keep.tile([P, PASSES, S], U8, name="v_scales", align_bytes=64)
+        nc.gpsimd.memset(v_scales[:].rearrange("p a c -> p (a c)").bitcast(I32), 0)
+        for q in range(QUADS):
+            first_row = ROW0 + 4 * PASSES * q
+            nc.sync.dma_start(
+                v_scales[32 * q : 32 * q + 4, :, :].bitcast(I32),
+                v_rows[first_row : first_row + 4 * PASSES, :].bitcast(I32),
+            )
+        table.append(load_table(2))
+        deal_words(1)
+        deal_words(2)
+
+        w4_planes = keep.tile([P, PASSES, H], U8, name="w4_planes", align_bytes=64)
+        for a in range(PASSES):
+            nc.vector.tensor_copy(
+                w4_planes[:, a, :].rearrange("p (t c) -> p t c", t=PACK),
+                w4_rows[:, a, :].rearrange("p (c t) -> p t c", t=PACK),
+            )
+
         minus_gains = keep.tile([P, GROUPS, PACK], F32, name="minus_gains")
         nc.gpsimd.tensor_scalar(minus_gains[:], gains[:], -1.0, 0.0, ALU.mult, ALU.add)
         slices = [(g, t) for g in range(GROUPS) for t in range(PACK)]
@@ -75,35 +115,6 @@ def tile_list_musette_reed_beating_kernel(
         for g, t in slices:
             pair[g, t] = keep.tile([P, PAIRS + SPARE], F32, name="pair%d%d" % (g, t))
             nc.gpsimd.memset(pair[g, t][:, PAIRS:], 0.0)
-
-        def spread_rows(queue, packed, name):
-            planes = keep.tile([P, PASSES, packed.shape[1]], U8, name=name, align_bytes=64)
-            nc.gpsimd.memset(planes[:].rearrange("p a c -> p (a c)").bitcast(I32), 0)
-            for q in range(QUADS):
-                first_row = ROW0 + 4 * PASSES * q
-                queue.dma_start(
-                    planes[32 * q : 32 * q + 4, :, :].bitcast(I32),
-                    packed[first_row : first_row + 4 * PASSES, :].bitcast(I32),
-                )
-            return planes
-
-        w4_dealt = keep.tile([P, H], U8, name="w4_dealt")
-        nc.vector.tensor_copy(
-            w4_dealt[:].rearrange("p (t c) -> p t c", t=PACK), w4_rows[:].rearrange("p (c t) -> p t c", t=PACK)
-        )
-        w4_planes = spread_rows(nc.gpsimd, w4_dealt, "w4_planes")
-        v_rows = keep.tile([P, S], U8, name="v_rows")
-        nc.vector.tensor_copy(v_rows[:], tab_rows[:].indirect(idx[:]))
-        v_scales = spread_rows(nc.scalar, v_rows, "v_scales")
-
-        w4_codes = [
-            keep.tile([P, 2 * H], U8, name="w4_codes%d" % a, tag="w4_codes%d" % a, align_bytes=64) for a in range(PASSES)
-        ]
-        for a in range(PASSES):
-            nc.vector.tensor_copy(
-                w4_codes[a][:].bitcast(U16).rearrange("p (t c) -> p t c", t=PACK),
-                w4_raw[:, a, :].bitcast(U16).rearrange("p (c t) -> p t c", t=PACK),
-            )
 
         v_words = []
         for a in range(PASSES):
@@ -118,7 +129,7 @@ def tile_list_musette_reed_beating_kernel(
 
         w2_raw = []
         for g in range(GROUPS):
-            raw = big.tile([P, PACK, H], F32, name="w2_raw%d" % g, tag="big", align_bytes=64)
+            raw = big.tile([P, PACK, H], F32, name="w2_raw%d" % g, tag="slot%d" % g, align_bytes=64)
             nc.sync.dma_start(raw[:], w2[g * K_PASS : (g + 1) * K_PASS, :].rearrange("(p j) n -> p j n", j=PACK))
             w2_raw.append(raw)
 
@@ -189,10 +200,10 @@ def tile_list_musette_reed_beating_kernel(
 
         y_codes = [keep.tile([P, S], U32, name="y_codes%d" % g, align_bytes=64) for g in range(GROUPS)]
         y_scales = [keep.tile([P, S], U8, name="y_scales%d" % g, align_bytes=64) for g in range(GROUPS)]
-        y_rows = out_0.rearrange("(g p t) j -> g t p j", g=GROUPS, t=PACK)
-        for g, j0, width in Y_PIECES:
+        y_rows = out_0.rearrange("(g p t) j -> g p t j", g=GROUPS, t=PACK)
+        for piece, (g, j0, width) in enumerate(Y_PIECES):
             cols = slice(j0, j0 + width)
-            y = big.tile([P, PACK, width], F32, name="y", tag="big", align_bytes=64)
+            y = big.tile([P, PACK, width], F32, name="y", tag="slot%d" % ((piece + 2) % 3), align_bytes=64)
             for t in range(PACK):
                 if j0 == 0:
                     acc = psum.tile([P, BANK], F32, name="acc2", tag="acc")
@@ -214,7 +225,7 @@ def tile_list_musette_reed_beating_kernel(
                     bounded[g, t][:, cols],
                     ALU.add,
                 )
-                nc.sync.dma_start(y_rows[g, t, :, cols], y[:, t, :])
+            nc.sync.dma_start(y_rows[g, :, :, cols], y[:])
             y_bf = stage.tile([P, width, PACK], BF16, name="y_bf", tag="stage", align_bytes=64)
             woven = y_bf[:].rearrange("p (c i) t -> p c t i", i=4)
             planes = y[:].rearrange("p t (c i) -> p c t i", i=4)

@@ -24,10 +24,22 @@ GROUPS = H // K_PASS
 BANK = 512
 QUADS = 4
 PER_COLUMN = 16
+RUN = 4
 SPARE = 32
 HALF = PAIRS // 2
 ROW0 = P - 16 * PASSES
 Y_PIECES = [(0, 0, 512), (0, 512, 512), (1, 0, 512), (1, 512, 256), (1, 768, 256)]
+
+
+def entries(start, stop):
+    return slice(start // PER_COLUMN, stop // PER_COLUMN)
+
+
+def weave(copy, woven, slices_of_group):
+    copy(
+        woven.rearrange("p (c i) t -> p c t i", i=RUN),
+        slices_of_group.rearrange("p t (c i) -> p c t i", i=RUN),
+    )
 
 
 def tile_list_musette_reed_beating_kernel(
@@ -38,14 +50,15 @@ def tile_list_musette_reed_beating_kernel(
         lists = ctx.enter_context(tc.tile_pool(name="lists", bufs=1))
         keep = ctx.enter_context(tc.tile_pool(name="keep", bufs=1))
         big = ctx.enter_context(tc.tile_pool(name="big", bufs=1))
-        rows = ctx.enter_context(tc.tile_pool(name="rows", bufs=8))
-        stage = ctx.enter_context(tc.tile_pool(name="stage", bufs=4))
+        rows = ctx.enter_context(tc.tile_pool(name="rows", bufs=GROUPS * PACK))
+        stage = ctx.enter_context(tc.tile_pool(name="stage", bufs=GROUPS * GROUPS))
         psum = ctx.enter_context(tc.psum_pool(name="psum", bufs=8))
 
         idx = lists.tile([P, S // PER_COLUMN], U16, name="idx")
         p1 = lists.tile([P, PAIRS // PER_COLUMN], U16, name="p1")
         p2 = lists.tile([P, PAIRS // PER_COLUMN], U16, name="p2")
         p3 = lists.tile([P, S // PER_COLUMN], U16, name="p3")
+
         tab_rows = big.tile([P, T], U8, name="tab_rows", tag="slot2", align_bytes=64)
         nc.vector.memset(tab_rows[:ROW0, :].bitcast(I32), 0)
         nc.scalar.dma_start(tab_rows[ROW0:, :].bitcast(I32), tab_scales.rearrange("a q c -> q a c").bitcast(I32))
@@ -68,8 +81,7 @@ def tile_list_musette_reed_beating_kernel(
         w4_rows = keep.tile([P, PASSES, H], U8, name="w4_rows")
         nc.gpsimd.memset(w4_rows[:].rearrange("p a c -> p (a c)").bitcast(I32), 0)
         for q in range(QUADS):
-            queue = nc.gpsimd if q == QUADS - 1 else nc.sync
-            queue.dma_start(
+            nc.sync.dma_start(
                 w4_rows[32 * q : 32 * q + 4, :, :].bitcast(I32),
                 w4_scales[:, 4 * q : 4 * q + 4, :].rearrange("a r c -> r a c").bitcast(I32),
             )
@@ -110,11 +122,11 @@ def tile_list_musette_reed_beating_kernel(
 
         minus_gains = keep.tile([P, GROUPS, PACK], F32, name="minus_gains")
         nc.gpsimd.tensor_scalar(minus_gains[:], gains[:], -1.0, 0.0, ALU.mult, ALU.add)
-        slices = [(g, t) for g in range(GROUPS) for t in range(PACK)]
         pair = {}
-        for g, t in slices:
-            pair[g, t] = keep.tile([P, PAIRS + SPARE], F32, name="pair%d%d" % (g, t))
-            nc.gpsimd.memset(pair[g, t][:, PAIRS:], 0.0)
+        for g in range(GROUPS):
+            for t in range(PACK):
+                pair[g, t] = keep.tile([P, PAIRS + SPARE], F32, name="pair%d%d" % (g, t))
+                nc.gpsimd.memset(pair[g, t][:, PAIRS:], 0.0)
 
         v_words = []
         for a in range(PASSES):
@@ -122,8 +134,7 @@ def tile_list_musette_reed_beating_kernel(
             width = BANK if a == PASSES - 1 else S
             for j0 in range(0, S, width):
                 nc.vector.tensor_copy(
-                    picked[:, j0 : j0 + width],
-                    table[a][:].bitcast(U32).indirect(idx[:, j0 // PER_COLUMN : (j0 + width) // PER_COLUMN]),
+                    picked[:, j0 : j0 + width], table[a][:].bitcast(U32).indirect(idx[:, entries(j0, j0 + width)])
                 )
             v_words.append(picked)
 
@@ -134,11 +145,12 @@ def tile_list_musette_reed_beating_kernel(
             w2_raw.append(raw)
 
         h, first = {}, {}
+        halves = [slice(m0, m0 + HALF) for m0 in range(0, PAIRS, HALF)]
         x_codes = [keep.tile([P, PAIRS], U32, name="x_codes%d" % g, align_bytes=64) for g in range(GROUPS)]
         x_scales = [keep.tile([P, PAIRS], U8, name="x_scales%d" % g, align_bytes=64) for g in range(GROUPS)]
         for g in range(GROUPS):
             first[g] = keep.tile([P, PACK, PAIRS], F32, name="first%d" % g)
-            second = keep.tile([P, PACK, PAIRS], F32, name="second%d" % g)
+            sums = keep.tile([P, PACK, PAIRS], F32, name="sums%d" % g)
             for t in range(PACK):
                 h[g, t] = keep.tile([P, S], F32, name="h%d%d" % (g, t))
                 c0 = (t * GROUPS + g) * P
@@ -155,26 +167,20 @@ def tile_list_musette_reed_beating_kernel(
                             stop=(a == PASSES - 1),
                         )
                     nc.scalar.copy(h[g, t][:, j0 : j0 + BANK], acc[:])
-                halves = [slice(m0, m0 + HALF) for m0 in range(0, PAIRS, HALF)]
                 for m in halves:
-                    entries = slice(m.start // PER_COLUMN, m.stop // PER_COLUMN)
-                    nc.vector.tensor_copy(first[g][:, t, m], h[g, t][:].indirect(p1[:, entries]))
+                    nc.vector.tensor_copy(first[g][:, t, m], h[g, t][:].indirect(p1[:, entries(m.start, m.stop)]))
                 for m in halves:
-                    entries = slice(m.start // PER_COLUMN, m.stop // PER_COLUMN)
                     nc.vector.tensor_tensor(
-                        second[:, t, m], h[g, t][:].indirect(p2[:, entries]), first[g][:, t, m], ALU.add
+                        sums[:, t, m], h[g, t][:].indirect(p2[:, entries(m.start, m.stop)]), first[g][:, t, m], ALU.add
                     )
-            x_bf = keep.tile([P, PAIRS, PACK], BF16, name="x_bf%d" % g, tag="w4_codes%d" % (2 if g == 0 else 9), align_bytes=64)
-            woven = x_bf[:].rearrange("p (c i) t -> p c t i", i=4)
-            planes = second[:].rearrange("p t (c i) -> p c t i", i=4)
-            if g == GROUPS - 1:
-                nc.vector.tensor_copy(woven, planes)
-            else:
-                nc.scalar.copy(woven, planes)
+            last = g == GROUPS - 1
+            x_tag = "x_last" if last else "w4_codes%d" % (PASSES - 1)
+            x_bf = keep.tile([P, PAIRS, PACK], BF16, name="x_bf%d" % g, tag=x_tag, align_bytes=64)
+            weave(nc.vector.tensor_copy if last else nc.scalar.copy, x_bf[:], sums[:])
             nc.vector.quantize_mx(x_codes[g][:].bitcast(FP8X4), x_scales[g][:], x_bf[:].rearrange("p m t -> p (m t)"))
             for m in halves:
                 nc.vector.scalar_tensor_tensor(
-                    first[g][:, :, m], first[g][:, :, m], -2.0, second[:, :, m], ALU.mult, ALU.add
+                    first[g][:, :, m], first[g][:, :, m], -2.0, sums[:, :, m], ALU.mult, ALU.add
                 )
 
         w2_codes, w2_scales = {}, {}
@@ -203,9 +209,9 @@ def tile_list_musette_reed_beating_kernel(
         y_rows = out_0.rearrange("(g p t) j -> g p t j", g=GROUPS, t=PACK)
         for piece, (g, j0, width) in enumerate(Y_PIECES):
             cols = slice(j0, j0 + width)
-            y = big.tile([P, PACK, width], F32, name="y", tag="slot%d" % ((piece + 2) % 3), align_bytes=64)
-            for t in range(PACK):
-                if j0 == 0:
+            y = big.tile([P, PACK, width], F32, name="y", tag="slot%d" % ((piece + GROUPS) % PASSES), align_bytes=64)
+            if j0 == 0:
+                for t in range(PACK):
                     acc = psum.tile([P, BANK], F32, name="acc2", tag="acc")
                     for r in range(GROUPS):
                         nc.tensor.matmul_mx(
@@ -220,19 +226,11 @@ def tile_list_musette_reed_beating_kernel(
                     nc.vector.tensor_tensor(pair[g, t][:, :PAIRS], acc[:], pair[g, t][:, :PAIRS], ALU.add)
             for t in range(PACK):
                 nc.vector.tensor_tensor(
-                    y[:, t, :],
-                    pair[g, t][:].indirect(p3[:, j0 // PER_COLUMN : (j0 + width) // PER_COLUMN]),
-                    bounded[g, t][:, cols],
-                    ALU.add,
+                    y[:, t, :], pair[g, t][:].indirect(p3[:, entries(j0, j0 + width)]), bounded[g, t][:, cols], ALU.add
                 )
             nc.sync.dma_start(y_rows[g, :, :, cols], y[:])
             y_bf = stage.tile([P, width, PACK], BF16, name="y_bf", tag="stage", align_bytes=64)
-            woven = y_bf[:].rearrange("p (c i) t -> p c t i", i=4)
-            planes = y[:].rearrange("p t (c i) -> p c t i", i=4)
-            if (g, j0, width) == Y_PIECES[-1]:
-                nc.vector.tensor_copy(woven, planes)
-            else:
-                nc.scalar.copy(woven, planes)
+            weave(nc.vector.tensor_copy if piece == len(Y_PIECES) - 1 else nc.scalar.copy, y_bf[:], y[:])
             nc.vector.quantize_mx(
                 y_codes[g][:, cols].bitcast(FP8X4), y_scales[g][:, cols], y_bf[:].rearrange("p m t -> p (m t)")
             )

from contextlib import ExitStack

import concourse.mybir as mybir

K, T, S, PAIRS, H = 1536, 4096, 1024, 512, 1024
FLOPS = 2 * K * H * S + 2 * H * H * PAIRS

F32 = mybir.dt.float32
BF16 = mybir.dt.bfloat16
I32 = mybir.dt.int32
U32 = mybir.dt.uint32
U16 = mybir.dt.uint16
U8 = mybir.dt.uint8
FP8X4 = mybir.dt.float8_e4m3fn_x4
FP4X4 = mybir.dt.float4_e2m1fn_x4
ACT = mybir.ActivationFunctionType
ALU = mybir.AluOpType

P = 128
PACK = 4
K_PASS = P * PACK
PASSES = K // K_PASS
GROUPS = H // K_PASS
BANK = 512
QUADS = 4
PER_COLUMN = 16
RUN = 4
SPARE = 32
HALF = PAIRS // 2
ROW0 = P - 16 * PASSES
Y_PIECES = [(0, 0, 512), (0, 512, 512), (1, 0, 512), (1, 512, 256), (1, 768, 256)]


def entries(start, stop):
    return slice(start // PER_COLUMN, stop // PER_COLUMN)


def weave(copy, woven, slices_of_group):
    copy(
        woven.rearrange("p (c i) t -> p c t i", i=RUN),
        slices_of_group.rearrange("p t (c i) -> p c t i", i=RUN),
    )


def tile_list_musette_reed_beating_kernel(
    tc, tab_words, tab_scales, offs, pos1, pos2, pos3, w4_words, w4_scales, w2, gain, out_0, out_1, out_2
):
    nc = tc.nc
    with ExitStack() as ctx:
        lists = ctx.enter_context(tc.tile_pool(name="lists", bufs=1))
        keep = ctx.enter_context(tc.tile_pool(name="keep", bufs=1))
        big = ctx.enter_context(tc.tile_pool(name="big", bufs=1))
        rows = ctx.enter_context(tc.tile_pool(name="rows", bufs=GROUPS * PACK))
        stage = ctx.enter_context(tc.tile_pool(name="stage", bufs=GROUPS * GROUPS))
        psum = ctx.enter_context(tc.psum_pool(name="psum", bufs=8))

        idx = lists.tile([P, S // PER_COLUMN], U16, name="idx")
        p1 = lists.tile([P, PAIRS // PER_COLUMN], U16, name="p1")
        p2 = lists.tile([P, PAIRS // PER_COLUMN], U16, name="p2")
        p3 = lists.tile([P, S // PER_COLUMN], U16, name="p3")

        tab_rows = big.tile([P, T], U8, name="tab_rows", tag="slot2", align_bytes=64)
        nc.vector.memset(tab_rows[:ROW0, :].bitcast(I32), 0)
        nc.scalar.dma_start(tab_rows[ROW0:, :].bitcast(I32), tab_scales.rearrange("a q c -> q a c").bitcast(I32))
        w4_first = big.tile([P, 2 * H], U8, name="w4_first", tag="slot1", align_bytes=64)
        nc.sync.dma_start(w4_first[:].bitcast(I32), w4_words[0].bitcast(I32))
        for tile, source in ((idx, offs), (p1, pos1), (p2, pos2), (p3, pos3)):
            nc.sync.dma_start(tile[:], source)
        gains = keep.tile([P, GROUPS, PACK], F32, name="gains")
        nc.sync.dma_start(gains[:], gain.rearrange("(g p t) -> p g t", g=GROUPS, t=PACK))

        def load_table(a):
            words = big.tile([P, T], I32, name="tab%d" % a, tag="slot%d" % a, align_bytes=64)
            nc.sync.dma_start(words[:], tab_words[a].rearrange("p t i -> p (t i)").bitcast(I32))
            return words

        table = [load_table(0)]
        w4_rest = stage.tile([P, PASSES - 1, 2 * H], U8, name="w4_rest", tag="stage", align_bytes=64)
        nc.sync.dma_start(w4_rest[:].bitcast(I32), w4_words[1:].rearrange("a p c -> p a c").bitcast(I32))
        w4_raw = [w4_first[:], w4_rest[:, 0, :], w4_rest[:, 1, :]]
        w4_rows = keep.tile([P, PASSES, H], U8, name="w4_rows")
        nc.gpsimd.memset(w4_rows[:].rearrange("p a c -> p (a c)").bitcast(I32), 0)
        for q in range(QUADS):
            nc.sync.dma_start(
                w4_rows[32 * q : 32 * q + 4, :, :].bitcast(I32),
                w4_scales[:, 4 * q : 4 * q + 4, :].rearrange("a r c -> r a c").bitcast(I32),
            )

        w4_codes = [
            keep.tile([P, 2 * H], U8, name="w4_codes%d" % a, tag="w4_codes%d" % a, align_bytes=64) for a in range(PASSES)
        ]

        def deal_words(a):
            nc.vector.tensor_copy(
                w4_codes[a][:].bitcast(U16).rearrange("p (t c) -> p t c", t=PACK),
                w4_raw[a].bitcast(U16).rearrange("p (c t) -> p t c", t=PACK),
            )

        deal_words(0)
        table.append(load_table(1))

        v_rows = keep.tile([P, S], U8, name="v_rows")
        nc.vector.tensor_copy(v_rows[:], tab_rows[:].indirect(idx[:]))
        v_scales = keep.tile([P, PASSES, S], U8, name="v_scales", align_bytes=64)
        nc.gpsimd.memset(v_scales[:].rearrange("p a c -> p (a c)").bitcast(I32), 0)
        for q in range(QUADS):
            first_row = ROW0 + 4 * PASSES * q
            nc.sync.dma_start(
                v_scales[32 * q : 32 * q + 4, :, :].bitcast(I32),
                v_rows[first_row : first_row + 4 * PASSES, :].bitcast(I32),
            )
        table.append(load_table(2))
        deal_words(1)
        deal_words(2)

        w4_planes = keep.tile([P, PASSES, H], U8, name="w4_planes", align_bytes=64)
        for a in range(PASSES):
            nc.vector.tensor_copy(
                w4_planes[:, a, :].rearrange("p (t c) -> p t c", t=PACK),
                w4_rows[:, a, :].rearrange("p (c t) -> p t c", t=PACK),
            )

        minus_gains = keep.tile([P, GROUPS, PACK], F32, name="minus_gains")
        nc.gpsimd.tensor_scalar(minus_gains[:], gains[:], -1.0, 0.0, ALU.mult, ALU.add)
        pair = {}
        for g in range(GROUPS):
            for t in range(PACK):
                pair[g, t] = keep.tile([P, PAIRS + SPARE], F32, name="pair%d%d" % (g, t))
                nc.gpsimd.memset(pair[g, t][:, PAIRS:], 0.0)

        v_words = []
        for a in range(PASSES):
            picked = rows.tile([P, S], U32, name="v_words%d" % a, tag="rows", align_bytes=64)
            width = BANK if a == PASSES - 1 else S
            for j0 in range(0, S, width):
                nc.vector.tensor_copy(
                    picked[:, j0 : j0 + width], table[a][:].bitcast(U32).indirect(idx[:, entries(j0, j0 + width)])
                )
            v_words.append(picked)

        w2_raw = []
        for g in range(GROUPS):
            raw = big.tile([P, PACK, H], F32, name="w2_raw%d" % g, tag="slot%d" % g, align_bytes=64)
            nc.sync.dma_start(raw[:], w2[g * K_PASS : (g + 1) * K_PASS, :].rearrange("(p j) n -> p j n", j=PACK))
            w2_raw.append(raw)

        h, first = {}, {}
        halves = [slice(m0, m0 + HALF) for m0 in range(0, PAIRS, HALF)]
        x_codes = [keep.tile([P, PAIRS], U32, name="x_codes%d" % g, align_bytes=64) for g in range(GROUPS)]
        x_scales = [keep.tile([P, PAIRS], U8, name="x_scales%d" % g, align_bytes=64) for g in range(GROUPS)]
        for g in range(GROUPS):
            first[g] = keep.tile([P, PACK, PAIRS], F32, name="first%d" % g)
            sums = keep.tile([P, PACK, PAIRS], F32, name="sums%d" % g)
            for t in range(PACK):
                h[g, t] = keep.tile([P, S], F32, name="h%d%d" % (g, t))
                c0 = (t * GROUPS + g) * P
                for j0 in range(0, S, BANK):
                    acc = psum.tile([P, BANK], F32, name="acc1", tag="acc")
                    for a in range(PASSES):
                        nc.tensor.matmul_mx(
                            acc[:],
                            lhsT=w4_codes[a][:, 2 * c0 : 2 * (c0 + P)].bitcast(FP4X4),
                            lhsT_scale=w4_planes[:, a, c0 : c0 + P],
                            rhs=v_words[a][:, j0 : j0 + BANK].bitcast(FP8X4),
                            rhs_scale=v_scales[:, a, j0 : j0 + BANK],
                            start=(a == 0),
                            stop=(a == PASSES - 1),
                        )
                    nc.scalar.copy(h[g, t][:, j0 : j0 + BANK], acc[:])
                for m in halves:
                    nc.vector.tensor_copy(first[g][:, t, m], h[g, t][:].indirect(p1[:, entries(m.start, m.stop)]))
                for m in halves:
                    nc.vector.tensor_tensor(
                        sums[:, t, m], h[g, t][:].indirect(p2[:, entries(m.start, m.stop)]), first[g][:, t, m], ALU.add
                    )
            last = g == GROUPS - 1
            x_tag = "x_last" if last else "w4_codes%d" % (PASSES - 1)
            x_bf = keep.tile([P, PAIRS, PACK], BF16, name="x_bf%d" % g, tag=x_tag, align_bytes=64)
            weave(nc.vector.tensor_copy if last else nc.scalar.copy, x_bf[:], sums[:])
            nc.vector.quantize_mx(x_codes[g][:].bitcast(FP8X4), x_scales[g][:], x_bf[:].rearrange("p m t -> p (m t)"))
            for m in halves:
                nc.vector.scalar_tensor_tensor(
                    first[g][:, :, m], first[g][:, :, m], -2.0, sums[:, :, m], ALU.mult, ALU.add
                )

        w2_codes, w2_scales = {}, {}
        for out_g in range(GROUPS):
            for g in range(GROUPS):
                w2_bf = stage.tile([P, PACK, P, PACK], BF16, name="w2_bf", tag="stage", align_bytes=64)
                nc.scalar.copy(
                    w2_bf[:].rearrange("p t m j -> p m j t"),
                    w2_raw[g][:, :, out_g * K_PASS : (out_g + 1) * K_PASS].rearrange("p j (m t) -> p m j t", t=PACK),
                )
                codes = keep.tile([P, K_PASS], U32, name="w2_codes%d%d" % (g, out_g), align_bytes=64)
                scales = keep.tile([P, K_PASS], U8, name="w2_scales%d%d" % (g, out_g), align_bytes=64)
                nc.vector.quantize_mx(codes[:].bitcast(FP8X4), scales[:], w2_bf[:].rearrange("p t m j -> p (t m j)"))
                w2_codes[g, out_g], w2_scales[g, out_g] = codes, scales

        bounded = {}
        for g in range(GROUPS):
            for t in range(PACK):
                nc.scalar.activation(pair[g, t][:, :PAIRS], first[g][:, t, :], ACT.Abs, scale=gains[:, g, t : t + 1])
            for t in range(PACK):
                bounded[g, t] = rows.tile([P, S], F32, name="bounded%d%d" % (g, t), tag="rows", align_bytes=64)
                nc.scalar.activation(bounded[g, t][:], h[g, t][:], ACT.Tanh, scale=minus_gains[:, g, t : t + 1])

        y_codes = [keep.tile([P, S], U32, name="y_codes%d" % g, align_bytes=64) for g in range(GROUPS)]
        y_scales = [keep.tile([P, S], U8, name="y_scales%d" % g, align_bytes=64) for g in range(GROUPS)]
        y_rows = out_0.rearrange("(g p t) j -> g p t j", g=GROUPS, t=PACK)
        for piece, (g, j0, width) in enumerate(Y_PIECES):
            cols = slice(j0, j0 + width)
            y = big.tile([P, PACK, width], F32, name="y", tag="slot%d" % ((piece + GROUPS) % PASSES), align_bytes=64)
            if j0 == 0:
                for t in range(PACK):
                    acc = psum.tile([P, BANK], F32, name="acc2", tag="acc")
                    for r in range(GROUPS):
                        nc.tensor.matmul_mx(
                            acc[:],
                            lhsT=w2_codes[r, g][:, t * P : (t + 1) * P].bitcast(FP8X4),
                            lhsT_scale=w2_scales[r, g][:, t * P : (t + 1) * P],
                            rhs=x_codes[r][:].bitcast(FP8X4),
                            rhs_scale=x_scales[r][:],
                            start=(r == 0),
                            stop=(r == GROUPS - 1),
                        )
                    nc.vector.tensor_tensor(pair[g, t][:, :PAIRS], acc[:], pair[g, t][:, :PAIRS], ALU.add)
            for t in range(PACK):
                nc.vector.tensor_tensor(
                    y[:, t, :], pair[g, t][:].indirect(p3[:, entries(j0, j0 + width)]), bounded[g, t][:, cols], ALU.add
                )
            nc.sync.dma_start(y_rows[g, :, :, cols], y[:])
            y_bf = stage.tile([P, width, PACK], BF16, name="y_bf", tag="stage", align_bytes=64)
            weave(nc.vector.tensor_copy if piece == len(Y_PIECES) - 1 else nc.scalar.copy, y_bf[:], y[:])
            nc.vector.quantize_mx(
                y_codes[g][:, cols].bitcast(FP8X4), y_scales[g][:, cols], y_bf[:].rearrange("p m t -> p (m t)")
            )
            nc.sync.dma_start(
                out_1[g].rearrange("p m t -> p (m t)").bitcast(I32)[:, cols], y_codes[g][:, cols].bitcast(I32)
            )
            if j0 + width == S:
                for q in range(QUADS):
                    queue = nc.scalar if q % 2 else nc.sync
                    queue.dma_start(
                        out_2[g, 4 * q : 4 * q + 4, :].bitcast(I32), y_scales[g][32 * q : 32 * q + 4, :].bitcast(I32)
                    )
